import numpy as np
import ml_dtypes


def mxq(x, axis, fmt="e4m3"):
    dtype, down = {"e4m3": (ml_dtypes.float8_e4m3fn, 7), "e5m2": (ml_dtypes.float8_e5m2, 14)}[fmt]
    v = np.moveaxis(np.asarray(x, np.float32).astype(ml_dtypes.bfloat16).astype(np.float64), axis, -1)
    blocks = v.reshape(v.shape[:-1] + (-1, 32))
    amax = np.abs(blocks).max(-1, keepdims=True)
    byte = np.maximum(np.where(amax > 0, np.frexp(amax)[1] - 1 + 127, 0) - down, 1)
    scale = np.exp2(byte - 127.0)
    codes = (blocks / scale).astype(np.float32).astype(dtype).astype(np.float64)
    return np.moveaxis((codes * scale).reshape(v.shape), -1, axis)


WIDE = False


def mx_kscale(k):
    if not WIDE:
        return np.ones(k)
    levels = np.array([10, -10, 5, -5, 0])
    if k % 512:
        return np.exp2(np.random.permutation(np.resize(levels, k // 32))).repeat(32)
    a = np.empty((k // 512, 16))
    for p in range(k // 512):
        a[p, :8] = np.random.permutation(np.resize(levels, 8))
        for g in range(8):
            far = levels[np.abs(levels - a[p, g]) >= 10]
            a[p, g + 8] = far[np.random.randint(len(far))]
    return np.exp2(a.ravel()).repeat(32)


def f64(x):
    return np.asarray(x).astype(np.float64)


def striped8(idx):
    return np.asarray(idx).reshape(8, -1, 16).transpose(0, 2, 1).reshape(128, -1).astype(np.uint16)


def unstriped8(offs):
    return offs.reshape(8, 16, -1).transpose(0, 2, 1).reshape(8, -1).astype(np.int64)


def pick8(x, idx, run):
    r = np.arange(len(x))
    return x[r[:, None], idx[r % (8 * run) // run]]


E2M1 = np.array([0.0, 0.5, 1.0, 1.5, 2.0, 3.0, 4.0, 6.0, -0.0, -0.5, -1.0, -1.5, -2.0, -3.0, -4.0, -6.0])


def pack_weight(w, fmt):
    k, n = w.shape
    w = f64(np.asarray(w, np.float32).astype(ml_dtypes.bfloat16)).reshape(k // 32, 32, n)
    amax = np.abs(w).max(1)
    if fmt == "e4m3":
        byte = np.frexp(amax)[1] - 1 + 127 - 7
    else:
        mant, ex = np.frexp(amax / 6.0)
        byte = np.where(mant > 0.5, ex, ex - 1) + 127
    byte = np.clip(np.where(amax > 0, byte, 1), 1, 254)
    scaled = (w * np.exp2(127.0 - byte)[:, None, :]).reshape(k, n).astype(np.float32)
    by_word = np.ascontiguousarray(scaled.reshape(k // 512, 128, 4, n).transpose(0, 1, 3, 2))
    if fmt == "e4m3":
        words = by_word.astype(ml_dtypes.float8_e4m3fn).view(np.uint8)
    else:
        c = by_word.astype(ml_dtypes.float4_e2m1fn).view(np.uint8) & 0xF
        words = (c[..., 0::2] | (c[..., 1::2] << 4)).reshape(k // 512, 128, 2 * n)
    return np.ascontiguousarray(words), np.ascontiguousarray(byte.astype(np.uint8).reshape(k // 512, 16, n))


def unpack_weight(words, scales, fmt):
    g, _, n = scales.shape
    words = np.ascontiguousarray(words).reshape(g, 128, n, -1)
    if fmt == "e4m3":
        vals = words.view(ml_dtypes.float8_e4m3fn).astype(np.float64)
    else:
        nib = np.empty((g, 128, n, 4), np.uint8)
        nib[..., 0::2] = words & 0xF
        nib[..., 1::2] = words >> 4
        vals = E2M1[nib]
    vals = vals * np.repeat(np.exp2(scales.astype(np.float64) - 127.0), 8, axis=1)[..., None]
    return vals.transpose(0, 1, 3, 2).reshape(g * 512, n)


D, K, T, U, I, Q = 512, 512, 1024, 1024, 512, 128


def setup_inputs():
    n = np.random.standard_normal
    idx = np.stack([np.random.permutation(T)[:I] for _ in range(8)])
    idx2 = np.stack([np.random.permutation(U)[:I] for _ in range(8)])
    idx3 = np.stack([np.random.permutation(T)[:I] for _ in range(8)])
    idx4 = np.stack([np.random.permutation(U)[:I] for _ in range(8)])
    fd = mx_kscale(D)
    fk = mx_kscale(K)
    wqp = pack_weight(n((D, K)) * 1.0 / np.sqrt(D) * fd[:, None] * fk, "e4m3")
    keysp = pack_weight(n((K, T)) * 1.0 / np.sqrt(K) / fk[:, None], "e4m3")
    notesp = pack_weight(n((D, U)) * 1.0 / np.sqrt(D) * fd[:, None], "e2m1")
    return {
        "states": (n((D, Q)) * 0.95 / fd[:, None]).astype(np.float32),
        "wq_words": wqp[0],
        "wq_scales": wqp[1],
        "keys_words": keysp[0],
        "keys_scales": keysp[1],
        "notes_words": notesp[0],
        "notes_scales": notesp[1],
        "offs": striped8(idx),
        "offs2": striped8(idx2),
        "offs3": striped8(idx3),
        "offs4": striped8(idx4),
    }


def reference(states, wq_words, wq_scales, keys_words, keys_scales, notes_words, notes_scales, offs, offs2, offs3, offs4):
    idx = unstriped8(offs)
    idx2 = unstriped8(offs2)
    idx3 = unstriped8(offs3)
    idx4 = unstriped8(offs4)
    wqu = unpack_weight(wq_words, wq_scales, "e4m3")
    keysu = unpack_weight(keys_words, keys_scales, "e4m3")
    notesu = unpack_weight(notes_words, notes_scales, "e2m1")
    statesq = mxq(f64(states), 0, "e4m3")
    qv = wqu.T @ statesq
    qvq = mxq(qv, 0, "e4m3")
    a = qvq.T @ keysu
    b = statesq.T @ notesu
    w = pick8(a, idx, 16) + pick8(b, idx2, 16)
    v = pick8(a, idx3, 16) - pick8(b, idx4, 16)
    f1 = np.zeros((Q, T))
    f1[np.arange(Q)[:, None], idx3[np.arange(Q) % 128 // 16]] = w
    f2 = np.zeros((Q, U))
    f2[np.arange(Q)[:, None], idx2[np.arange(Q) % 128 // 16]] = v
    aa = a - f1
    bb = b + f2
    y = np.maximum(pick8(aa, idx, 16), pick8(bb, idx4, 16))
    return y

@@ -1,0 +1,173 @@
+from contextlib import ExitStack
+
+import concourse.mybir as mybir
+
+F32 = mybir.dt.float32
+BF16 = mybir.dt.bfloat16
+I32 = mybir.dt.int32
+U32 = mybir.dt.uint32
+U16 = mybir.dt.uint16
+U8 = mybir.dt.uint8
+FP8X4 = mybir.dt.float8_e4m3fn_x4
+FP4X4 = mybir.dt.float4_e2m1fn_x4
+ADD = mybir.AluOpType.add
+SUB = mybir.AluOpType.subtract
+MULT = mybir.AluOpType.mult
+MAX = mybir.AluOpType.max
+COPY = mybir.ActivationFunctionType.Copy
+
+P = 128
+PACK = 4
+D, K, T, U, SLOTS, Q = 512, 512, 1024, 1024, 512, 128
+HALF = SLOTS // 2
+LIST_COLS = SLOTS // 16
+FLOPS = 2 * Q * (D * K + K * T + D * U)
+
+
+def load_scale_rows(queue, plane, rows, quads):
+    for quad in quads:
+        queue.dma_start(
+            out=plane[32 * quad : 32 * quad + 4, :].bitcast(I32),
+            in_=rows[0, 4 * quad : 4 * quad + 4, :].bitcast(I32),
+        )
+
+
+def tile_attend_crossbook_madeside_kernel(
+    tc, states, wq_words, wq_scales, keys_words, keys_scales, notes_words, notes_scales, offs, offs2, offs3, offs4, out
+):
+    nc = tc.nc
+    with ExitStack() as ctx:
+        keep = ctx.enter_context(tc.tile_pool(name="keep", bufs=1))
+        psum = ctx.enter_context(tc.psum_pool(name="psum", bufs=1))
+
+        wq_plane_raw = keep.tile([P, K], U8, align_bytes=64)
+        notes_plane = keep.tile([P, U], U8, align_bytes=64)
+        keys_plane = keep.tile([P, T], U8, align_bytes=64)
+        for plane in (wq_plane_raw, notes_plane, keys_plane):
+            nc.vector.memset(plane[:].bitcast(I32), 0)
+        f1 = keep.tile([P, T], F32)
+        f2 = keep.tile([P, U], F32)
+        nc.vector.memset(f1[:], 0.0)
+        nc.vector.memset(f2[:], 0.0)
+
+        states_raw = keep.tile([P, PACK, Q], F32)
+        nc.sync.dma_start(out=states_raw[:], in_=states.rearrange("(p j) q -> p j q", j=PACK))
+        load_scale_rows(nc.sync, wq_plane_raw, wq_scales, range(4))
+        wq_raw = keep.tile([P, K], U32, align_bytes=64)
+        nc.sync.dma_start(out=wq_raw[:].bitcast(I32), in_=wq_words[0].rearrange("p c r -> p (c r)").bitcast(I32))
+        notes_codes = keep.tile([P, 2 * U], U8, align_bytes=64)
+        nc.sync.dma_start(out=notes_codes[:].bitcast(I32), in_=notes_words[0].bitcast(I32))
+        keys_src = keys_words[0].rearrange("p c r -> p (c r)").bitcast(I32)
+        keys_codes = [keep.tile([P, T // 2], U32, align_bytes=64, name="keys_codes", tag="keys%d" % n) for n in range(2)]
+        nc.sync.dma_start(out=keys_codes[0][:].bitcast(I32), in_=keys_src[:, 0 : T // 2])
+        load_scale_rows(nc.sync, notes_plane, notes_scales, range(4))
+        nc.sync.dma_start(out=keys_codes[1][:].bitcast(I32), in_=keys_src[:, T // 2 : T])
+        load_scale_rows(nc.sync, keys_plane, keys_scales, (0, 1))
+        load_scale_rows(nc.gpsimd, keys_plane, keys_scales, (2, 3))
+        lists = {}
+        for name, src in (("idx2", offs2), ("idx", offs), ("idx4", offs4), ("idx3", offs3)):
+            lists[name] = keep.tile([P, LIST_COLS], U16, name=name)
+            nc.sync.dma_start(lists[name][:], src)
+
+        def half_list(name, h):
+            return lists[name][:, h * LIST_COLS // 2 : (h + 1) * LIST_COLS // 2]
+
+        def half(t, h):
+            return t[:, h * HALF : (h + 1) * HALF]
+
+        states_bf = keep.tile([P, Q, PACK], BF16, align_bytes=64)
+        dst = states_bf[:].rearrange("p (c i) j -> p c j i", i=4)
+        src = states_raw[:].rearrange("p j (c i) -> p c j i", i=4)
+        nc.scalar.activation(dst[:, 0:12], src[:, 0:12], COPY)
+        nc.vector.tensor_copy(dst[:, 12:32], src[:, 12:32])
+        wq_plane = keep.tile([P, K], U8, align_bytes=64)
+        plane_dst = wq_plane[:].rearrange("p (j m) -> p j m", j=PACK)
+        plane_src = wq_plane_raw[:].rearrange("p (m j) -> p j m", j=PACK)
+        nc.vector.tensor_copy(plane_dst[:, 0:2], plane_src[:, 0:2])
+        s_codes = keep.tile([P, Q], U32, align_bytes=64)
+        s_plane = keep.tile([P, Q], U8, align_bytes=64)
+        nc.vector.quantize_mx(
+            out=s_codes[:].bitcast(FP8X4), scales=s_plane[:], in_=states_bf[:].rearrange("p q j -> p (q j)")
+        )
+        nc.vector.tensor_copy(plane_dst[:, 2:4], plane_src[:, 2:4])
+        wq_codes = keep.tile([P, K], U32, align_bytes=64)
+        codes_dst = wq_codes[:].rearrange("p (j c i) -> p c j i", j=PACK, i=4)
+        codes_src = wq_raw[:].rearrange("p (c i j) -> p c j i", j=PACK, i=4)
+        for j in range(PACK):
+            nc.scalar.copy(codes_dst[:, :, j], codes_src[:, :, j])
+
+        qv_ps = psum.tile([P, PACK, Q], F32, tag="bank7")
+        for j in range(PACK):
+            cols = slice(j * P, (j + 1) * P)
+            nc.tensor.matmul_mx(
+                out=qv_ps[:, j, :], lhsT=wq_codes[:, cols].bitcast(FP8X4), lhsT_scale=wq_plane[:, cols],
+                rhs=s_codes[:].bitcast(FP8X4), rhs_scale=s_plane[:], start=True, stop=True,
+            )
+        b_ps = [psum.tile([P, 256], F32, name="b_ps%d" % n, tag="bank%d" % n) for n in range(4)]
+        for n in range(4):
+            nc.tensor.matmul_mx(
+                out=b_ps[n][:], lhsT=s_codes[:].bitcast(FP8X4), lhsT_scale=s_plane[:],
+                rhs=notes_codes[:, 512 * n : 512 * (n + 1)].bitcast(FP4X4),
+                rhs_scale=notes_plane[:, 256 * n : 256 * (n + 1)], start=True, stop=True,
+            )
+        qv_bf = keep.tile([P, Q, PACK], BF16, align_bytes=64)
+        nc.scalar.activation(qv_bf[:], qv_ps[:].rearrange("p j q -> p q j"), COPY)
+        b_sb = keep.tile([P, U], F32)
+        nc.vector.tensor_copy(b_sb[:, 0:256], b_ps[0][:])
+        q_codes = keep.tile([P, Q], U32, align_bytes=64)
+        q_plane = keep.tile([P, Q], U8, align_bytes=64)
+        nc.vector.quantize_mx(
+            out=q_codes[:].bitcast(FP8X4), scales=q_plane[:], in_=qv_bf[:].rearrange("p q j -> p (q j)")
+        )
+        nc.scalar.copy(b_sb[:, 256:512], b_ps[1][:])
+        nc.vector.tensor_copy(b_sb[:, 512:768], b_ps[2][:])
+        nc.scalar.copy(b_sb[:, 768:1024], b_ps[3][:])
+
+        a_ps = [psum.tile([P, 256], F32, name="a_ps%d" % n, tag="bank%d" % (4 + n)) for n in range(4)]
+        a_sb = keep.tile([P, T], F32)
+        for n in range(4):
+            cols = slice(256 * n, 256 * (n + 1))
+            nc.tensor.matmul_mx(
+                out=a_ps[n][:], lhsT=q_codes[:].bitcast(FP8X4), lhsT_scale=q_plane[:],
+                rhs=keys_codes[n // 2][:, 256 * (n % 2) : 256 * (n % 2 + 1)].bitcast(FP8X4), rhs_scale=keys_plane[:, cols], start=True, stop=True,
+            )
+        def pick(window, name, h, tag, scale=1.0):
+            picked = keep.tile([P, HALF], F32, align_bytes=64, name=tag, tag=tag)
+            nc.scalar.activation(picked[:], window[:].indirect(half_list(name, h)), COPY, scale=scale)
+            return picked
+
+        b2 = pick(b_sb, "idx2", 0, "b2")
+        for n in range(4):
+            if n == 2:
+                nc.scalar.copy(a_sb[:, 256 * n : 256 * (n + 1)], a_ps[n][:])
+            else:
+                nc.vector.tensor_copy(a_sb[:, 256 * n : 256 * (n + 1)], a_ps[n][:])
+        minus_b4 = keep.tile([P, HALF], F32, align_bytes=64, tag="keys1")
+        nc.vector.tensor_scalar(minus_b4[:], b_sb[:].indirect(half_list("idx4", 0)), -1.0, 0.0, MULT, ADD)
+        a1 = [pick(a_sb, "idx", 0, "a1_first")]
+        a3 = [pick(a_sb, "idx3", 0, "a3_first")]
+        a1.append(pick(a_sb, "idx", 1, "a1_second"))
+        a3.append(pick(a_sb, "idx3", 1, "a3_second"))
+        nc.vector.tensor_tensor(f1[:].indirect(half_list("idx3", 0)), a1[0][:], b2[:], ADD)
+        b2 = pick(b_sb, "idx2", 1, "b2")
+        nc.vector.tensor_tensor(f2[:].indirect(half_list("idx2", 0)), a3[0][:], minus_b4[:], ADD)
+        minus_b4 = pick(b_sb, "idx4", 1, "keys1", -1.0)
+        nc.vector.tensor_tensor(f1[:].indirect(half_list("idx3", 1)), a1[1][:], b2[:], ADD)
+        nc.vector.tensor_tensor(f2[:].indirect(half_list("idx2", 1)), a3[1][:], minus_b4[:], ADD)
+
+        aa = keep.tile([P, T], F32)
+        bb = keep.tile([P, U], F32)
+        for whole, banks, copy, placed, op in ((aa, a_ps, a_sb, f1, SUB), (bb, b_ps, b_sb, f2, ADD)):
+            for n in range(3):
+                cols = slice(256 * n, 256 * (n + 1))
+                nc.vector.tensor_tensor(whole[:, cols], banks[n][:], placed[:, cols], op)
+            nc.gpsimd.tensor_tensor(whole[:, 768:1024], copy[:, 768:1024], placed[:, 768:1024], op)
+        aa1 = keep.tile([P, SLOTS], F32)
+        bb4 = keep.tile([P, SLOTS], F32)
+        nc.scalar.activation(aa1[:], aa[:].indirect(lists["idx"][:]), COPY)
+        nc.vector.tensor_copy(half(bb4, 0), bb[:].indirect(half_list("idx4", 0)))
+        nc.scalar.activation(half(bb4, 1), bb[:].indirect(half_list("idx4", 1)), COPY)
+        best = keep.tile([P, SLOTS], F32)
+        for h, queue in ((0, nc.sync), (1, nc.scalar)):
+            nc.vector.tensor_tensor(half(best, h), half(aa1, h), half(bb4, h), MAX)
+            queue.dma_start(out=out[:, h * HALF : (h + 1) * HALF], in_=half(best, h))

@@ -40,34 +40,38 @@ def tile_attend_crossbook_madeside_kernel(
         keep = ctx.enter_context(tc.tile_pool(name="keep", bufs=1))
         psum = ctx.enter_context(tc.psum_pool(name="psum", bufs=1))
 
-        wq_plane_raw = keep.tile([P, K], U8, align_bytes=64)
+        wq_plane_raw = keep.tile([P, K], U8, align_bytes=64, tag="plane_then_f2")
         notes_plane = keep.tile([P, U], U8, align_bytes=64)
         keys_plane = keep.tile([P, T], U8, align_bytes=64)
         for plane in (wq_plane_raw, notes_plane, keys_plane):
             nc.vector.memset(plane[:].bitcast(I32), 0)
-        f1 = keep.tile([P, T], F32)
-        f2 = keep.tile([P, U], F32)
-        nc.vector.memset(f1[:], 0.0)
-        nc.vector.memset(f2[:], 0.0)
 
         states_raw = keep.tile([P, PACK, Q], F32)
         nc.sync.dma_start(out=states_raw[:], in_=states.rearrange("(p j) q -> p j q", j=PACK))
-        load_scale_rows(nc.sync, wq_plane_raw, wq_scales, range(4))
+        load_scale_rows(nc.sync, wq_plane_raw, wq_scales, (0, 1))
         wq_raw = keep.tile([P, K], U32, align_bytes=64)
         nc.sync.dma_start(out=wq_raw[:].bitcast(I32), in_=wq_words[0].rearrange("p c r -> p (c r)").bitcast(I32))
+        load_scale_rows(nc.sync, wq_plane_raw, wq_scales, (2, 3))
         notes_codes = keep.tile([P, 2 * U], U8, align_bytes=64)
         nc.sync.dma_start(out=notes_codes[:].bitcast(I32), in_=notes_words[0].bitcast(I32))
         keys_src = keys_words[0].rearrange("p c r -> p (c r)").bitcast(I32)
         keys_codes = [keep.tile([P, T // 2], U32, align_bytes=64, name="keys_codes", tag="keys%d" % n) for n in range(2)]
         nc.sync.dma_start(out=keys_codes[0][:].bitcast(I32), in_=keys_src[:, 0 : T // 2])
-        load_scale_rows(nc.sync, notes_plane, notes_scales, range(4))
+        load_scale_rows(nc.sync, notes_plane, notes_scales, (0, 1, 2))
+        load_scale_rows(nc.gpsimd, notes_plane, notes_scales, (3,))
         nc.sync.dma_start(out=keys_codes[1][:].bitcast(I32), in_=keys_src[:, T // 2 : T])
-        load_scale_rows(nc.sync, keys_plane, keys_scales, (0, 1))
-        load_scale_rows(nc.gpsimd, keys_plane, keys_scales, (2, 3))
         lists = {}
-        for name, src in (("idx2", offs2), ("idx", offs), ("idx4", offs4), ("idx3", offs3)):
+
+        def load_list(name, src):
             lists[name] = keep.tile([P, LIST_COLS], U16, name=name)
             nc.sync.dma_start(lists[name][:], src)
+
+        load_scale_rows(nc.sync, keys_plane, keys_scales, (0, 1, 2))
+        load_scale_rows(nc.gpsimd, keys_plane, keys_scales, (3,))
+        load_list("idx2", offs2)
+        load_list("idx", offs)
+        load_list("idx4", offs4)
+        load_list("idx3", offs3)
 
         def half_list(name, h):
             return lists[name][:, h * LIST_COLS // 2 : (h + 1) * LIST_COLS // 2]
@@ -83,24 +87,26 @@ def tile_attend_crossbook_madeside_kernel(
         wq_plane = keep.tile([P, K], U8, align_bytes=64)
         plane_dst = wq_plane[:].rearrange("p (j m) -> p j m", j=PACK)
         plane_src = wq_plane_raw[:].rearrange("p (m j) -> p j m", j=PACK)
-        nc.vector.tensor_copy(plane_dst[:, 0:2], plane_src[:, 0:2])
         s_codes = keep.tile([P, Q], U32, align_bytes=64)
         s_plane = keep.tile([P, Q], U8, align_bytes=64)
         nc.vector.quantize_mx(
             out=s_codes[:].bitcast(FP8X4), scales=s_plane[:], in_=states_bf[:].rearrange("p q j -> p (q j)")
         )
+        nc.vector.tensor_copy(plane_dst[:, 0:2], plane_src[:, 0:2])
         nc.vector.tensor_copy(plane_dst[:, 2:4], plane_src[:, 2:4])
-        wq_codes = keep.tile([P, K], U32, align_bytes=64)
+        wq_codes = keep.tile([P, K], U32, align_bytes=64, tag="wq_then_f1")
         codes_dst = wq_codes[:].rearrange("p (j c i) -> p c j i", j=PACK, i=4)
         codes_src = wq_raw[:].rearrange("p (c i j) -> p c j i", j=PACK, i=4)
-        for j in range(PACK):
-            nc.scalar.copy(codes_dst[:, :, j], codes_src[:, :, j])
+        nc.scalar.copy(codes_dst[:, :, 0:2], codes_src[:, :, 0:2])
+        nc.scalar.copy(codes_dst[:, :, 2:4], codes_src[:, :, 2:4])
+        f2 = keep.tile([P, U], F32, align_bytes=64, tag="plane_then_f2")
+        nc.vector.memset(f2[:], 0.0)
 
-        qv_ps = psum.tile([P, PACK, Q], F32, tag="bank7")
+        qv_ps = [psum.tile([P, 2, Q], F32, name="qv_ps", tag="bank%d" % (6 + n)) for n in range(2)]
         for j in range(PACK):
             cols = slice(j * P, (j + 1) * P)
             nc.tensor.matmul_mx(
-                out=qv_ps[:, j, :], lhsT=wq_codes[:, cols].bitcast(FP8X4), lhsT_scale=wq_plane[:, cols],
+                out=qv_ps[j // 2][:, j % 2, :], lhsT=wq_codes[:, cols].bitcast(FP8X4), lhsT_scale=wq_plane[:, cols],
                 rhs=s_codes[:].bitcast(FP8X4), rhs_scale=s_plane[:], start=True, stop=True,
             )
         b_ps = [psum.tile([P, 256], F32, name="b_ps%d" % n, tag="bank%d" % n) for n in range(4)]
@@ -111,7 +117,10 @@ def tile_attend_crossbook_madeside_kernel(
                 rhs_scale=notes_plane[:, 256 * n : 256 * (n + 1)], start=True, stop=True,
             )
         qv_bf = keep.tile([P, Q, PACK], BF16, align_bytes=64)
-        nc.scalar.activation(qv_bf[:], qv_ps[:].rearrange("p j q -> p q j"), COPY)
+        nc.vector.tensor_copy(qv_bf[:, :, 0:2], qv_ps[0][:].rearrange("p j q -> p q j"))
+        nc.scalar.activation(qv_bf[:, :, 2:4], qv_ps[1][:].rearrange("p j q -> p q j"), COPY)
+        f1 = keep.tile([P, T], F32, align_bytes=64, tag="wq_then_f1")
+        nc.vector.memset(f1[:], 0.0)
         b_sb = keep.tile([P, U], F32)
         nc.vector.tensor_copy(b_sb[:, 0:256], b_ps[0][:])
         q_codes = keep.tile([P, Q], U32, align_bytes=64)

@@ -94,7 +94,7 @@ def tile_attend_crossbook_madeside_kernel(
         )
         nc.vector.tensor_copy(plane_dst[:, 0:2], plane_src[:, 0:2])
         nc.vector.tensor_copy(plane_dst[:, 2:4], plane_src[:, 2:4])
-        wq_codes = keep.tile([P, K], U32, align_bytes=64, tag="wq_then_f1")
+        wq_codes = keep.tile([P, K], U32, align_bytes=64)
         codes_dst = wq_codes[:].rearrange("p (j c i) -> p c j i", j=PACK, i=4)
         codes_src = wq_raw[:].rearrange("p (c i j) -> p c j i", j=PACK, i=4)
         nc.scalar.copy(codes_dst[:, :, 0:2], codes_src[:, :, 0:2])
@@ -116,11 +116,9 @@ def tile_attend_crossbook_madeside_kernel(
                 rhs=notes_codes[:, 512 * n : 512 * (n + 1)].bitcast(FP4X4),
                 rhs_scale=notes_plane[:, 256 * n : 256 * (n + 1)], start=True, stop=True,
             )
-        qv_bf = keep.tile([P, Q, PACK], BF16, align_bytes=64)
+        qv_bf = keep.tile([P, Q, PACK], BF16, align_bytes=64, tag="qv_then_f1")
         nc.vector.tensor_copy(qv_bf[:, :, 0:2], qv_ps[0][:].rearrange("p j q -> p q j"))
         nc.scalar.activation(qv_bf[:, :, 2:4], qv_ps[1][:].rearrange("p j q -> p q j"), COPY)
-        f1 = keep.tile([P, T], F32, align_bytes=64, tag="wq_then_f1")
-        nc.vector.memset(f1[:], 0.0)
         b_sb = keep.tile([P, U], F32)
         nc.vector.tensor_copy(b_sb[:, 0:256], b_ps[0][:])
         q_codes = keep.tile([P, Q], U32, align_bytes=64)
@@ -128,6 +126,8 @@ def tile_attend_crossbook_madeside_kernel(
         nc.vector.quantize_mx(
             out=q_codes[:].bitcast(FP8X4), scales=q_plane[:], in_=qv_bf[:].rearrange("p q j -> p (q j)")
         )
+        f1 = keep.tile([P, T], F32, align_bytes=64, tag="qv_then_f1")
+        nc.gpsimd.memset(f1[:], 0.0)
         nc.scalar.copy(b_sb[:, 256:512], b_ps[1][:])
         nc.vector.tensor_copy(b_sb[:, 512:768], b_ps[2][:])
         nc.scalar.copy(b_sb[:, 768:1024], b_ps[3][:])

@@ -140,9 +140,9 @@ def tile_attend_crossbook_madeside_kernel(
                 out=a_ps[n][:], lhsT=q_codes[:].bitcast(FP8X4), lhsT_scale=q_plane[:],
                 rhs=keys_codes[n // 2][:, 256 * (n % 2) : 256 * (n % 2 + 1)].bitcast(FP8X4), rhs_scale=keys_plane[:, cols], start=True, stop=True,
             )
-        def pick(window, name, h, tag, scale=1.0):
+        def pick(window, name, h, tag):
             picked = keep.tile([P, HALF], F32, align_bytes=64, name=tag, tag=tag)
-            nc.scalar.activation(picked[:], window[:].indirect(half_list(name, h)), COPY, scale=scale)
+            nc.scalar.activation(picked[:], window[:].indirect(half_list(name, h)), COPY)
             return picked
 
         b2 = pick(b_sb, "idx2", 0, "b2")
@@ -153,24 +153,27 @@ def tile_attend_crossbook_madeside_kernel(
                 nc.vector.tensor_copy(a_sb[:, 256 * n : 256 * (n + 1)], a_ps[n][:])
         minus_b4 = keep.tile([P, HALF], F32, align_bytes=64, tag="keys1")
         nc.vector.tensor_scalar(minus_b4[:], b_sb[:].indirect(half_list("idx4", 0)), -1.0, 0.0, MULT, ADD)
-        a1 = [pick(a_sb, "idx", 0, "a1_first")]
-        a3 = [pick(a_sb, "idx3", 0, "a3_first")]
-        a1.append(pick(a_sb, "idx", 1, "a1_second"))
-        a3.append(pick(a_sb, "idx3", 1, "a3_second"))
-        nc.vector.tensor_tensor(f1[:].indirect(half_list("idx3", 0)), a1[0][:], b2[:], ADD)
-        b2 = pick(b_sb, "idx2", 1, "b2")
-        nc.vector.tensor_tensor(f2[:].indirect(half_list("idx2", 0)), a3[0][:], minus_b4[:], ADD)
-        minus_b4 = pick(b_sb, "idx4", 1, "keys1", -1.0)
-        nc.vector.tensor_tensor(f1[:].indirect(half_list("idx3", 1)), a1[1][:], b2[:], ADD)
-        nc.vector.tensor_tensor(f2[:].indirect(half_list("idx2", 1)), a3[1][:], minus_b4[:], ADD)
+        a1 = pick(a_sb, "idx", 0, "a1_then_b4")
+        a3 = pick(a_sb, "idx3", 0, "a3_first")
+        a1_second = pick(a_sb, "idx", 1, "a1_second")
+        a3_second = pick(a_sb, "idx3", 1, "a3_second")
+        nc.vector.tensor_tensor(f1[:].indirect(half_list("idx3", 0)), a1[:], b2[:], ADD)
+        b4_second = pick(b_sb, "idx4", 1, "a1_then_b4")
+        b2_second = pick(b_sb, "idx2", 1, "b2")
+        nc.vector.tensor_tensor(f2[:].indirect(half_list("idx2", 0)), a3[:], minus_b4[:], ADD)
+        v_second = keep.tile([P, HALF], F32)
+        nc.vector.tensor_tensor(v_second[:], a3_second[:], b4_second[:], SUB)
+        nc.vector.tensor_tensor(f1[:].indirect(half_list("idx3", 1)), a1_second[:], b2_second[:], ADD)
+        nc.vector.tensor_copy(f2[:].indirect(half_list("idx2", 1)), v_second[:])
 
         aa = keep.tile([P, T], F32)
         bb = keep.tile([P, U], F32)
-        for whole, banks, copy, placed, op in ((aa, a_ps, a_sb, f1, SUB), (bb, b_ps, b_sb, f2, ADD)):
-            for n in range(3):
-                cols = slice(256 * n, 256 * (n + 1))
-                nc.vector.tensor_tensor(whole[:, cols], banks[n][:], placed[:, cols], op)
-            nc.gpsimd.tensor_tensor(whole[:, 768:1024], copy[:, 768:1024], placed[:, 768:1024], op)
+        nc.gpsimd.tensor_tensor(aa[:, 256:1024], a_sb[:, 256:1024], f1[:, 256:1024], SUB)
+        nc.vector.tensor_tensor(aa[:, 0:256], a_ps[0][:], f1[:, 0:256], SUB)
+        for n in range(3):
+            cols = slice(256 * n, 256 * (n + 1))
+            nc.vector.tensor_tensor(bb[:, cols], b_ps[n][:], f2[:, cols], ADD)
+        nc.gpsimd.tensor_tensor(bb[:, 768:1024], b_sb[:, 768:1024], f2[:, 768:1024], ADD)
         aa1 = keep.tile([P, SLOTS], F32)
         bb4 = keep.tile([P, SLOTS], F32)
         nc.scalar.activation(aa1[:], aa[:].indirect(lists["idx"][:]), COPY)

from contextlib import ExitStack

import concourse.mybir as mybir

F32 = mybir.dt.float32
BF16 = mybir.dt.bfloat16
I32 = mybir.dt.int32
U32 = mybir.dt.uint32
U16 = mybir.dt.uint16
U8 = mybir.dt.uint8
FP8X4 = mybir.dt.float8_e4m3fn_x4
FP4X4 = mybir.dt.float4_e2m1fn_x4
ADD = mybir.AluOpType.add
SUB = mybir.AluOpType.subtract
MULT = mybir.AluOpType.mult
MAX = mybir.AluOpType.max
COPY = mybir.ActivationFunctionType.Copy

P = 128
PACK = 4
D, K, T, U, SLOTS, Q = 512, 512, 1024, 1024, 512, 128
HALF = SLOTS // 2
LIST_COLS = SLOTS // 16
FLOPS = 2 * Q * (D * K + K * T + D * U)


def load_scale_rows(queue, plane, rows, quads):
    for quad in quads:
        queue.dma_start(
            out=plane[32 * quad : 32 * quad + 4, :].bitcast(I32),
            in_=rows[0, 4 * quad : 4 * quad + 4, :].bitcast(I32),
        )


def tile_attend_crossbook_madeside_kernel(
    tc, states, wq_words, wq_scales, keys_words, keys_scales, notes_words, notes_scales, offs, offs2, offs3, offs4, out
):
    nc = tc.nc
    with ExitStack() as ctx:
        keep = ctx.enter_context(tc.tile_pool(name="keep", bufs=1))
        psum = ctx.enter_context(tc.psum_pool(name="psum", bufs=1))

        wq_plane_raw = keep.tile([P, K], U8, align_bytes=64, tag="plane_then_f2")
        notes_plane = keep.tile([P, U], U8, align_bytes=64)
        keys_plane = keep.tile([P, T], U8, align_bytes=64)
        for plane in (wq_plane_raw, notes_plane, keys_plane):
            nc.vector.memset(plane[:].bitcast(I32), 0)

        states_raw = keep.tile([P, PACK, Q], F32)
        nc.sync.dma_start(out=states_raw[:], in_=states.rearrange("(p j) q -> p j q", j=PACK))
        load_scale_rows(nc.sync, wq_plane_raw, wq_scales, (0, 1))
        wq_raw = keep.tile([P, K], U32, align_bytes=64)
        nc.sync.dma_start(out=wq_raw[:].bitcast(I32), in_=wq_words[0].rearrange("p c r -> p (c r)").bitcast(I32))
        load_scale_rows(nc.sync, wq_plane_raw, wq_scales, (2, 3))
        notes_codes = keep.tile([P, 2 * U], U8, align_bytes=64)
        nc.sync.dma_start(out=notes_codes[:].bitcast(I32), in_=notes_words[0].bitcast(I32))
        keys_src = keys_words[0].rearrange("p c r -> p (c r)").bitcast(I32)
        keys_codes = [keep.tile([P, T // 2], U32, align_bytes=64, name="keys_codes", tag="keys%d" % n) for n in range(2)]
        nc.sync.dma_start(out=keys_codes[0][:].bitcast(I32), in_=keys_src[:, 0 : T // 2])
        load_scale_rows(nc.sync, notes_plane, notes_scales, (0, 1, 2))
        load_scale_rows(nc.gpsimd, notes_plane, notes_scales, (3,))
        nc.sync.dma_start(out=keys_codes[1][:].bitcast(I32), in_=keys_src[:, T // 2 : T])
        lists = {}

        def load_list(name, src):
            lists[name] = keep.tile([P, LIST_COLS], U16, name=name)
            nc.sync.dma_start(lists[name][:], src)

        load_scale_rows(nc.sync, keys_plane, keys_scales, (0, 1, 2))
        load_scale_rows(nc.gpsimd, keys_plane, keys_scales, (3,))
        load_list("idx2", offs2)
        load_list("idx", offs)
        load_list("idx4", offs4)
        load_list("idx3", offs3)

        def half_list(name, h):
            return lists[name][:, h * LIST_COLS // 2 : (h + 1) * LIST_COLS // 2]

        def half(t, h):
            return t[:, h * HALF : (h + 1) * HALF]

        states_bf = keep.tile([P, Q, PACK], BF16, align_bytes=64)
        dst = states_bf[:].rearrange("p (c i) j -> p c j i", i=4)
        src = states_raw[:].rearrange("p j (c i) -> p c j i", i=4)
        nc.scalar.activation(dst[:, 0:12], src[:, 0:12], COPY)
        nc.vector.tensor_copy(dst[:, 12:32], src[:, 12:32])
        wq_plane = keep.tile([P, K], U8, align_bytes=64)
        plane_dst = wq_plane[:].rearrange("p (j m) -> p j m", j=PACK)
        plane_src = wq_plane_raw[:].rearrange("p (m j) -> p j m", j=PACK)
        s_codes = keep.tile([P, Q], U32, align_bytes=64)
        s_plane = keep.tile([P, Q], U8, align_bytes=64)
        nc.vector.quantize_mx(
            out=s_codes[:].bitcast(FP8X4), scales=s_plane[:], in_=states_bf[:].rearrange("p q j -> p (q j)")
        )
        nc.vector.tensor_copy(plane_dst[:, 0:2], plane_src[:, 0:2])
        nc.vector.tensor_copy(plane_dst[:, 2:4], plane_src[:, 2:4])
        wq_codes = keep.tile([P, K], U32, align_bytes=64)
        codes_dst = wq_codes[:].rearrange("p (j c i) -> p c j i", j=PACK, i=4)
        codes_src = wq_raw[:].rearrange("p (c i j) -> p c j i", j=PACK, i=4)
        nc.scalar.copy(codes_dst[:, :, 0:2], codes_src[:, :, 0:2])
        nc.scalar.copy(codes_dst[:, :, 2:4], codes_src[:, :, 2:4])
        f2 = keep.tile([P, U], F32, align_bytes=64, tag="plane_then_f2")
        nc.vector.memset(f2[:], 0.0)

        qv_ps = [psum.tile([P, 2, Q], F32, name="qv_ps", tag="bank%d" % (6 + n)) for n in range(2)]
        for j in range(PACK):
            cols = slice(j * P, (j + 1) * P)
            nc.tensor.matmul_mx(
                out=qv_ps[j // 2][:, j % 2, :], lhsT=wq_codes[:, cols].bitcast(FP8X4), lhsT_scale=wq_plane[:, cols],
                rhs=s_codes[:].bitcast(FP8X4), rhs_scale=s_plane[:], start=True, stop=True,
            )
        b_ps = [psum.tile([P, 256], F32, name="b_ps%d" % n, tag="bank%d" % n) for n in range(4)]
        for n in range(4):
            nc.tensor.matmul_mx(
                out=b_ps[n][:], lhsT=s_codes[:].bitcast(FP8X4), lhsT_scale=s_plane[:],
                rhs=notes_codes[:, 512 * n : 512 * (n + 1)].bitcast(FP4X4),
                rhs_scale=notes_plane[:, 256 * n : 256 * (n + 1)], start=True, stop=True,
            )
        qv_bf = keep.tile([P, Q, PACK], BF16, align_bytes=64, tag="qv_then_f1")
        nc.vector.tensor_copy(qv_bf[:, :, 0:2], qv_ps[0][:].rearrange("p j q -> p q j"))
        nc.scalar.activation(qv_bf[:, :, 2:4], qv_ps[1][:].rearrange("p j q -> p q j"), COPY)
        b_sb = keep.tile([P, U], F32)
        nc.vector.tensor_copy(b_sb[:, 0:256], b_ps[0][:])
        q_codes = keep.tile([P, Q], U32, align_bytes=64)
        q_plane = keep.tile([P, Q], U8, align_bytes=64)
        nc.vector.quantize_mx(
            out=q_codes[:].bitcast(FP8X4), scales=q_plane[:], in_=qv_bf[:].rearrange("p q j -> p (q j)")
        )
        f1 = keep.tile([P, T], F32, align_bytes=64, tag="qv_then_f1")
        nc.gpsimd.memset(f1[:], 0.0)
        nc.scalar.copy(b_sb[:, 256:512], b_ps[1][:])
        nc.vector.tensor_copy(b_sb[:, 512:768], b_ps[2][:])
        nc.scalar.copy(b_sb[:, 768:1024], b_ps[3][:])

        a_ps = [psum.tile([P, 256], F32, name="a_ps%d" % n, tag="bank%d" % (4 + n)) for n in range(4)]
        a_sb = keep.tile([P, T], F32)
        for n in range(4):
            cols = slice(256 * n, 256 * (n + 1))
            nc.tensor.matmul_mx(
                out=a_ps[n][:], lhsT=q_codes[:].bitcast(FP8X4), lhsT_scale=q_plane[:],
                rhs=keys_codes[n // 2][:, 256 * (n % 2) : 256 * (n % 2 + 1)].bitcast(FP8X4), rhs_scale=keys_plane[:, cols], start=True, stop=True,
            )
        def pick(window, name, h, tag):
            picked = keep.tile([P, HALF], F32, align_bytes=64, name=tag, tag=tag)
            nc.scalar.activation(picked[:], window[:].indirect(half_list(name, h)), COPY)
            return picked

        b2 = pick(b_sb, "idx2", 0, "b2")
        for n in range(4):
            if n == 2:
                nc.scalar.copy(a_sb[:, 256 * n : 256 * (n + 1)], a_ps[n][:])
            else:
                nc.vector.tensor_copy(a_sb[:, 256 * n : 256 * (n + 1)], a_ps[n][:])
        minus_b4 = keep.tile([P, HALF], F32, align_bytes=64, tag="keys1")
        nc.vector.tensor_scalar(minus_b4[:], b_sb[:].indirect(half_list("idx4", 0)), -1.0, 0.0, MULT, ADD)
        a1 = pick(a_sb, "idx", 0, "a1_then_b4")
        a3 = pick(a_sb, "idx3", 0, "a3_first")
        a1_second = pick(a_sb, "idx", 1, "a1_second")
        a3_second = pick(a_sb, "idx3", 1, "a3_second")
        nc.vector.tensor_tensor(f1[:].indirect(half_list("idx3", 0)), a1[:], b2[:], ADD)
        b4_second = pick(b_sb, "idx4", 1, "a1_then_b4")
        b2_second = pick(b_sb, "idx2", 1, "b2")
        nc.vector.tensor_tensor(f2[:].indirect(half_list("idx2", 0)), a3[:], minus_b4[:], ADD)
        v_second = keep.tile([P, HALF], F32)
        nc.vector.tensor_tensor(v_second[:], a3_second[:], b4_second[:], SUB)
        nc.vector.tensor_tensor(f1[:].indirect(half_list("idx3", 1)), a1_second[:], b2_second[:], ADD)
        nc.vector.tensor_copy(f2[:].indirect(half_list("idx2", 1)), v_second[:])

        aa = keep.tile([P, T], F32)
        bb = keep.tile([P, U], F32)
        nc.gpsimd.tensor_tensor(aa[:, 256:1024], a_sb[:, 256:1024], f1[:, 256:1024], SUB)
        nc.vector.tensor_tensor(aa[:, 0:256], a_ps[0][:], f1[:, 0:256], SUB)
        for n in range(3):
            cols = slice(256 * n, 256 * (n + 1))
            nc.vector.tensor_tensor(bb[:, cols], b_ps[n][:], f2[:, cols], ADD)
        nc.gpsimd.tensor_tensor(bb[:, 768:1024], b_sb[:, 768:1024], f2[:, 768:1024], ADD)
        aa1 = keep.tile([P, SLOTS], F32)
        bb4 = keep.tile([P, SLOTS], F32)
        nc.scalar.activation(aa1[:], aa[:].indirect(lists["idx"][:]), COPY)
        nc.vector.tensor_copy(half(bb4, 0), bb[:].indirect(half_list("idx4", 0)))
        nc.scalar.activation(half(bb4, 1), bb[:].indirect(half_list("idx4", 1)), COPY)
        best = keep.tile([P, SLOTS], F32)
        for h, queue in ((0, nc.sync), (1, nc.scalar)):
            nc.vector.tensor_tensor(half(best, h), half(aa1, h), half(bb4, h), MAX)
            queue.dma_start(out=out[:, h * HALF : (h + 1) * HALF], in_=half(best, h))
